import numpy as np
import ml_dtypes


def mxq(x, axis, fmt="e4m3"):
    dtype, down = {"e4m3": (ml_dtypes.float8_e4m3fn, 7), "e5m2": (ml_dtypes.float8_e5m2, 14)}[fmt]
    v = np.moveaxis(np.asarray(x, np.float32).astype(ml_dtypes.bfloat16).astype(np.float64), axis, -1)
    blocks = v.reshape(v.shape[:-1] + (-1, 32))
    amax = np.abs(blocks).max(-1, keepdims=True)
    byte = np.maximum(np.where(amax > 0, np.frexp(amax)[1] - 1 + 127, 0) - down, 1)
    scale = np.exp2(byte - 127.0)
    codes = (blocks / scale).astype(np.float32).astype(dtype).astype(np.float64)
    return np.moveaxis((codes * scale).reshape(v.shape), -1, axis)


WIDE = False


def mx_kscale(k):
    if not WIDE:
        return np.ones(k)
    levels = np.array([10, -10, 5, -5, 0])
    if k % 512:
        return np.exp2(np.random.permutation(np.resize(levels, k // 32))).repeat(32)
    a = np.empty((k // 512, 16))
    for p in range(k // 512):
        a[p, :8] = np.random.permutation(np.resize(levels, 8))
        for g in range(8):
            far = levels[np.abs(levels - a[p, g]) >= 10]
            a[p, g + 8] = far[np.random.randint(len(far))]
    return np.exp2(a.ravel()).repeat(32)


def f64(x):
    return np.asarray(x).astype(np.float64)


def striped(idx):
    return np.tile(idx.reshape(-1, 16).T, (8, 1)).astype(np.uint16)


def unstriped(offs):
    return offs[:16].T.reshape(-1).astype(np.int64)


def pack_weight(w):
    k, n = w.shape
    w = f64(np.asarray(w, np.float32).astype(ml_dtypes.bfloat16)).reshape(k // 32, 32, n)
    amax = np.abs(w).max(1)
    byte = np.clip(np.where(amax > 0, np.frexp(amax)[1] - 1 + 127 - 7, 1), 1, 254)
    scaled = (w * np.exp2(127.0 - byte)[:, None, :]).reshape(k, n).astype(np.float32)
    words = np.ascontiguousarray(scaled.reshape(k // 512, 128, 4, n).transpose(0, 1, 3, 2)).astype(ml_dtypes.float8_e4m3fn).view(np.uint8)
    return words, np.ascontiguousarray(byte.astype(np.uint8).reshape(k // 512, 16, n))


def unpack_weight(words, scales):
    g, p, n, _ = words.shape
    vals = np.ascontiguousarray(words).view(ml_dtypes.float8_e4m3fn).astype(np.float64) * np.repeat(np.exp2(scales.astype(np.float64) - 127.0), 8, axis=1)[..., None]
    return vals.transpose(0, 1, 3, 2).reshape(g * 512, n)


K, T, S, N, H = 1024, 2048, 512, 256, 512


def setup_inputs():
    n = np.random.standard_normal
    s = mx_kscale(K)[:, None]
    u = mx_kscale(H)
    packed_xT = pack_weight(n((K, T)) * s)
    return {
        "x_words": packed_xT[0],
        "x_scales": packed_xT[1],
        "w1": (n((K, H)) / np.sqrt(K) / s).astype(np.float32),
        "w2": (n((K, H)) / np.sqrt(K) / s).astype(np.float32),
        "bx": (np.random.uniform(0.3, 0.9, (H, 1))).astype(np.float32),
        "gx": (np.random.uniform(0.3, 0.9, (H, 1))).astype(np.float32),
        "unit": (np.random.uniform(0.6, 1.4, (H, 1)) * u[:, None]).astype(np.float32),
        "w3": (n((H, N)) / np.sqrt(H) / u[:, None]).astype(np.float32),
        "offs": striped(np.random.permutation(T)[:S]),
        "prv": striped(np.random.permutation(S)),
        "coh": striped(np.random.permutation(S)),
    }


def reference(x_words, x_scales, w1, w2, bx, gx, unit, w3, offs, prv, coh):
    xq = unpack_weight(x_words, x_scales)[:, unstriped(offs)]
    kt = mxq(f64(w1), 0, "e4m3").T @ xq
    ya = mxq(f64(w2), 0, "e4m3").T @ xq
    gc = ya[:, unstriped(coh)]
    lm = f64(bx) * kt + f64(gx) * gc
    mx = np.exp(1.2 * np.tanh(lm))
    qx = -1.0 * np.exp(-1.0 * mx) + 1.0
    kp = kt[:, unstriped(prv)]
    dk = kt - kp
    hid = f64(unit) * (qx * dk)
    return mxq(f64(w3), 0, "e4m3").T @ mxq(hid, 0, "e4m3")

@@ -1,0 +1,236 @@
+from contextlib import ExitStack
+
+import concourse.mybir as mybir
+
+K, T, S, N, H = 1024, 2048, 512, 256, 512
+FLOPS = 2 * K * H * S * 2 + 2 * H * N * S
+
+F32 = mybir.dt.float32
+BF16 = mybir.dt.bfloat16
+I32 = mybir.dt.int32
+U32 = mybir.dt.uint32
+U16 = mybir.dt.uint16
+U8 = mybir.dt.uint8
+FP8X4 = mybir.dt.float8_e4m3fn_x4
+ACT = mybir.ActivationFunctionType
+ALU = mybir.AluOpType
+
+P = 128
+PACK = 4
+K_PASS = P * PACK
+PASSES = K // K_PASS
+LIST_COL = 16
+HALF = S // 2
+CHUNK = 128
+SLOTS = [(e, h) for e in range(2) for h in range(2)]
+
+
+def tile_picked_yleeca_imp_p_kernel(tc, x_words, x_scales, w1, w2, bx, gx, unit, w3, offs, prv, coh, out):
+    nc = tc.nc
+    with ExitStack() as ctx:
+        lists = ctx.enter_context(tc.tile_pool(name="lists", bufs=1))
+        keep = ctx.enter_context(tc.tile_pool(name="keep", bufs=1))
+        work = ctx.enter_context(tc.tile_pool(name="work", bufs=S // CHUNK))
+        psum = ctx.enter_context(tc.psum_pool(name="psum", bufs=1))
+
+        def load_list(name, source):
+            tile = lists.tile([P, S // LIST_COL], U16, name=name)
+            nc.sync.dma_start(tile[:], source)
+            return tile
+
+        def load_rows(name, rows):
+            raw = keep.tile([P, PACK, rows.shape[1]], F32, name=name, tag=name)
+            nc.sync.dma_start(raw[:], rows.rearrange("(p j) c -> p j c", j=PACK))
+            return raw
+
+        def load_words(o):
+            table = keep.tile([P, T], U32, name="x_table%d" % o)
+            nc.sync.dma_start(table[:].bitcast(I32), x_words[o].rearrange("p c r -> p (c r)").bitcast(I32))
+            return table
+
+        def load_factor(name, column):
+            tile = keep.tile([P, PACK], F32, name=name, tag=name)
+            nc.sync.dma_start(tile[:], column.rearrange("(p t) o -> p (t o)", t=PACK))
+            return tile
+
+        def quantize(pool, name, grouped, width):
+            codes = pool.tile([P, width], U32, name=name + "_codes", align_bytes=64)
+            scales = pool.tile([P, width], U8, name=name + "_scales", align_bytes=64)
+            nc.vector.quantize_mx(out=codes[:].bitcast(FP8X4), scales=scales[:], in_=grouped[:])
+            return codes, scales
+
+        def copy_on_scalar(out, in_):
+            nc.scalar.activation(out, in_, ACT.Copy)
+
+        def quantize_dealt(name, raw, copy):
+            grouped = keep.tile([P, H * PACK], BF16, name=name + "_grouped", align_bytes=64)
+            copy(
+                grouped[:].rearrange("p (t m j) -> p m j t", t=PACK, j=PACK),
+                raw[:].rearrange("p j (m t) -> p m j t", t=PACK),
+            )
+            return quantize(keep, name, grouped, H)
+
+        scale_table = keep.tile([P, T], U8, name="scale_table")
+        nc.gpsimd.memset(scale_table[:].bitcast(I32), 0)
+        w1_raw = [load_rows("w1_raw0", w1[:K_PASS, :])]
+        for q in range(4):
+            nc.sync.dma_start(
+                scale_table[32 * q : 32 * q + 4 * PASSES, :].bitcast(I32),
+                x_scales[:, 4 * q : 4 * q + 4, :].bitcast(I32),
+            )
+        offs_sb = load_list("offs_sb", offs)
+        w1_raw.append(load_rows("w1_raw1", w1[K_PASS:, :]))
+        x_tables = [load_words(o) for o in range(PASSES)]
+        unit_sb = load_factor("unit_sb", unit)
+        prv_sb = load_list("prv_sb", prv)
+        w2_raw = [load_rows("w2_raw0", w2[:K_PASS, :])]
+        gx_sb = load_factor("gx_sb", gx)
+        bx_sb = load_factor("bx_sb", bx)
+        w2_raw.append(load_rows("w2_raw1", w2[K_PASS:, :]))
+        coh_sb = load_list("coh_sb", coh)
+        w3_raw = load_rows("w3_raw", w3)
+
+        x_planes = keep.tile([P, S], U8, name="x_planes", align_bytes=64)
+        nc.vector.tensor_copy(x_planes[:], scale_table[:].indirect(offs_sb[:]))
+        w1_mx = [
+            quantize_dealt("w1_0", w1_raw[0], copy_on_scalar),
+            quantize_dealt("w1_1", w1_raw[1], nc.vector.tensor_copy),
+        ]
+        x_codes = []
+        for o in range(PASSES):
+            picked = keep.tile([P, S], U32, name="x_codes%d" % o, align_bytes=64)
+            nc.vector.tensor_copy(picked[:], x_tables[o][:].indirect(offs_sb[:]))
+            x_codes.append(picked)
+
+        def product_pass(banks, w_mx, o):
+            codes, scales = w_mx
+            for e, h in SLOTS:
+                t = 2 * h + e
+                cols = slice(t * P, (t + 1) * P)
+                nc.tensor.matmul_mx(
+                    out=banks[t][:],
+                    lhsT=codes[:, cols].bitcast(FP8X4),
+                    lhsT_scale=scales[:, cols],
+                    rhs=x_codes[o][:].bitcast(FP8X4),
+                    rhs_scale=x_planes[4 * o : P, :],
+                    start=(o == 0),
+                    stop=(o == PASSES - 1),
+                )
+
+        kt_banks = [psum.tile([P, S], F32, name="kt%d" % t) for t in range(PACK)]
+        for o in range(PASSES):
+            product_pass(kt_banks, w1_mx[o], o)
+
+        ukt = [keep.tile([P, 2 * S], F32, name="ukt%d" % e) for e in range(2)]
+        for e, h in SLOTS:
+            t = 2 * h + e
+            nc.scalar.activation(ukt[e][:, h * S : (h + 1) * S], kt_banks[t][:], ACT.Copy, scale=unit_sb[:, t : t + 1])
+
+        def fetch_previous(e, tag):
+            ukp = keep.tile([P, 2 * S], F32, name="ukp%d" % e, tag=tag)
+            for h in range(2):
+                for j0 in range(0, S, HALF):
+                    nc.scalar.activation(
+                        ukp[:, h * S + j0 : h * S + j0 + HALF],
+                        ukt[e][:, h * S : (h + 1) * S].indirect(prv_sb[:, j0 // LIST_COL : (j0 + HALF) // LIST_COL]),
+                        ACT.Copy,
+                    )
+            return ukp
+
+        def subtract(e, ukp):
+            nc.vector.tensor_tensor(
+                ndk[:, e, :].rearrange("p (j h) -> p j h", h=2),
+                ukp[:].rearrange("p (h j) -> p j h", h=2),
+                ukt[e][:].rearrange("p (h j) -> p j h", h=2),
+                ALU.subtract,
+            )
+
+        ukp0 = fetch_previous(0, "ukp0")
+
+        ya_banks = [psum.tile([P, S], F32, name="ya%d" % t, tag="ya%d" % t) for t in range(PACK)]
+        for o in range(PASSES):
+            product_pass(ya_banks, quantize_dealt("w2_%d" % o, w2_raw[o], nc.vector.tensor_copy), o)
+
+        w3_grouped = keep.tile([P, N * PACK], BF16, name="w3_grouped", align_bytes=64)
+        nc.vector.tensor_copy(
+            out=w3_grouped[:].rearrange("p (c i j) -> p c j i", i=4, j=PACK),
+            in_=w3_raw[:].rearrange("p j (c i) -> p c j i", i=4),
+        )
+        w3_codes, w3_scales = quantize(keep, "w3", w3_grouped, N)
+
+        ndk = keep.tile([P, 2, 2 * S], F32, name="ndk", tag="w2_raw1")
+        subtract(0, ukp0)
+
+        gya = [keep.tile([P, S], F32, name="gya%d" % t) for t in range(PACK)]
+        for e, h in SLOTS:
+            t = 2 * h + e
+            nc.scalar.activation(gya[t][:], ya_banks[t][:], ACT.Copy, scale=gx_sb[:, t : t + 1])
+
+        ukp1 = fetch_previous(1, "gx_sb")
+
+        def rates(j0):
+            cols = slice(j0, j0 + CHUNK)
+            gc = work.tile([P, PACK * CHUNK], F32, name="gc")
+            lm = work.tile([P, PACK * CHUNK], F32, name="lm")
+            for u, (e, h) in enumerate(SLOTS):
+                nc.vector.tensor_copy(
+                    gc[:, u * CHUNK : (u + 1) * CHUNK],
+                    gya[2 * h + e][:].indirect(coh_sb[:, j0 // LIST_COL : (j0 + CHUNK) // LIST_COL]),
+                )
+            for u, (e, h) in enumerate(SLOTS):
+                t = 2 * h + e
+                part = slice(u * CHUNK, (u + 1) * CHUNK)
+                nc.vector.scalar_tensor_tensor(
+                    lm[:, part], kt_banks[t][:, cols], bx_sb[:, t : t + 1], gc[:, part], ALU.mult, ALU.add
+                )
+            th = work.tile([P, PACK * CHUNK], F32, name="th")
+            nc.scalar.activation(
+                th[:].rearrange("p (e j h) -> p e j h", e=2, h=2),
+                lm[:].rearrange("p (e h j) -> p e j h", e=2, h=2),
+                ACT.Tanh,
+            )
+            mx = work.tile([P, PACK * CHUNK], F32, name="mx")
+            nc.scalar.activation(mx[:], th[:], ACT.Exp, scale=1.2)
+            alive = work.tile([P, PACK * CHUNK], F32, name="alive")
+            nc.scalar.activation(
+                alive[:].rearrange("p (m e) -> p m e", e=2),
+                mx[:].rearrange("p (e m) -> p m e", e=2),
+                ACT.Exp,
+                scale=-1.0,
+            )
+            return alive
+
+        def finish(c, j0, alive):
+            cols = slice(j0, j0 + CHUNK)
+            hid = work.tile([P, PACK * CHUNK], BF16, name="hid", align_bytes=64)
+            nc.vector.scalar_tensor_tensor(
+                hid[:].rearrange("p (m e) -> p m e", e=2),
+                alive[:].rearrange("p (m e) -> p m e", e=2),
+                1.0,
+                ndk[:, :, 2 * j0 : 2 * (j0 + CHUNK)].rearrange("p e m -> p m e"),
+                ALU.subtract,
+                ALU.mult,
+            )
+            hid_codes, hid_scales = quantize(work, "hid", hid, CHUNK)
+            acc = psum.tile([P, N // P, CHUNK], F32, name="acc%d" % c, tag="ya%d" % c)
+            for r in range(N // P):
+                rows = slice(r * P, (r + 1) * P)
+                nc.tensor.matmul_mx(
+                    out=acc[:, r, :],
+                    lhsT=w3_codes[:, rows].bitcast(FP8X4),
+                    lhsT_scale=w3_scales[:, rows],
+                    rhs=hid_codes[:].bitcast(FP8X4),
+                    rhs_scale=hid_scales[:],
+                    start=True,
+                    stop=True,
+                )
+            result = work.tile([P, N // P, CHUNK], F32, name="result")
+            nc.scalar.copy(result[:], acc[:])
+            nc.sync.dma_start(out[:, cols].rearrange("(r p) j -> p r j", p=P), result[:])
+
+        starts = list(range(0, S, CHUNK))
+        alives = [rates(j0) for j0 in starts[:2]]
+        subtract(1, ukp1)
+        alives.extend([rates(j0) for j0 in starts[2:]])
+        for c, j0 in enumerate(starts):
+            finish(c, j0, alives[c])

@@ -21,7 +21,7 @@ K_PASS = P * PACK
 PASSES = K // K_PASS
 LIST_COL = 16
 HALF = S // 2
-CHUNK = 128
+CHUNKS = [256,128,64,64]
 SLOTS = [(e, h) for e in range(2) for h in range(2)]
 
 
@@ -30,7 +30,7 @@ def tile_picked_yleeca_imp_p_kernel(tc, x_words, x_scales, w1, w2, bx, gx, unit,
     with ExitStack() as ctx:
         lists = ctx.enter_context(tc.tile_pool(name="lists", bufs=1))
         keep = ctx.enter_context(tc.tile_pool(name="keep", bufs=1))
-        work = ctx.enter_context(tc.tile_pool(name="work", bufs=S // CHUNK))
+        work = ctx.enter_context(tc.tile_pool(name="work", bufs=len(CHUNKS)))
         psum = ctx.enter_context(tc.psum_pool(name="psum", bufs=1))
 
         def load_list(name, source):
@@ -61,6 +61,12 @@ def tile_picked_yleeca_imp_p_kernel(tc, x_words, x_scales, w1, w2, bx, gx, unit,
 
         def copy_on_scalar(out, in_):
             nc.scalar.activation(out, in_, ACT.Copy)
+
+        def scale_out_of_bank(on_vector, out_tile, bank, factor):
+            if on_vector:
+                nc.vector.tensor_scalar(out_tile, bank, factor, None, ALU.mult)
+            else:
+                nc.scalar.activation(out_tile, bank, ACT.Copy, scale=factor)
 
         def quantize_dealt(name, raw, copy):
             grouped = keep.tile([P, H * PACK], BF16, name=name + "_grouped", align_bytes=64)
@@ -93,8 +99,8 @@ def tile_picked_yleeca_imp_p_kernel(tc, x_words, x_scales, w1, w2, bx, gx, unit,
         x_planes = keep.tile([P, S], U8, name="x_planes", align_bytes=64)
         nc.vector.tensor_copy(x_planes[:], scale_table[:].indirect(offs_sb[:]))
         w1_mx = [
-            quantize_dealt("w1_0", w1_raw[0], copy_on_scalar),
-            quantize_dealt("w1_1", w1_raw[1], nc.vector.tensor_copy),
+            quantize_dealt("w1_0", w1_raw[0], nc.vector.tensor_copy),
+            quantize_dealt("w1_1", w1_raw[1], copy_on_scalar),
         ]
         x_codes = []
         for o in range(PASSES):
@@ -138,7 +144,7 @@ def tile_picked_yleeca_imp_p_kernel(tc, x_words, x_scales, w1, w2, bx, gx, unit,
             return ukp
 
         def subtract(e, ukp):
-            nc.vector.tensor_tensor(
+            [nc.gpsimd,nc.gpsimd][e].tensor_tensor(
                 ndk[:, e, :].rearrange("p (j h) -> p j h", h=2),
                 ukp[:].rearrange("p (h j) -> p j h", h=2),
                 ukt[e][:].rearrange("p (h j) -> p j h", h=2),
@@ -158,40 +164,50 @@ def tile_picked_yleeca_imp_p_kernel(tc, x_words, x_scales, w1, w2, bx, gx, unit,
         )
         w3_codes, w3_scales = quantize(keep, "w3", w3_grouped, N)
 
-        ndk = keep.tile([P, 2, 2 * S], F32, name="ndk", tag="w2_raw1")
+        ndk = keep.tile([P, 2, 2 * S], F32, name="ndk")
         subtract(0, ukp0)
 
         gya = [keep.tile([P, S], F32, name="gya%d" % t) for t in range(PACK)]
         for e, h in SLOTS:
             t = 2 * h + e
-            nc.scalar.activation(gya[t][:], ya_banks[t][:], ACT.Copy, scale=gx_sb[:, t : t + 1])
+            scale_out_of_bank(t in [0], gya[t][:], ya_banks[t][:], gx_sb[:, t : t + 1])
 
         ukp1 = fetch_previous(1, "gx_sb")
 
-        def rates(j0):
-            cols = slice(j0, j0 + CHUNK)
-            gc = work.tile([P, PACK * CHUNK], F32, name="gc")
-            lm = work.tile([P, PACK * CHUNK], F32, name="lm")
-            for u, (e, h) in enumerate(SLOTS):
-                nc.vector.tensor_copy(
-                    gc[:, u * CHUNK : (u + 1) * CHUNK],
-                    gya[2 * h + e][:].indirect(coh_sb[:, j0 // LIST_COL : (j0 + CHUNK) // LIST_COL]),
-                )
+        starts = [sum(CHUNKS[:c]) for c in range(len(CHUNKS))]
+
+        def logits(c):
+            j0, n = starts[c], CHUNKS[c]
+            gc = work.tile([P, PACK * n], F32, name="gc")
+            lm = work.tile([P, PACK * n], F32, name="lm")
             for u, (e, h) in enumerate(SLOTS):
                 t = 2 * h + e
-                part = slice(u * CHUNK, (u + 1) * CHUNK)
+                copy = copy_on_scalar if (c, t) in [] else nc.vector.tensor_copy
+                copy(gc[:, u * n : (u + 1) * n], gya[t][:].indirect(coh_sb[:, j0 // LIST_COL : (j0 + n) // LIST_COL]))
+            for u, (e, h) in enumerate(SLOTS):
+                t = 2 * h + e
+                part = slice(u * n, (u + 1) * n)
                 nc.vector.scalar_tensor_tensor(
-                    lm[:, part], kt_banks[t][:, cols], bx_sb[:, t : t + 1], gc[:, part], ALU.mult, ALU.add
+                    lm[:, part], kt_banks[t][:, j0 : j0 + n], bx_sb[:, t : t + 1], gc[:, part], ALU.mult, ALU.add
                 )
-            th = work.tile([P, PACK * CHUNK], F32, name="th")
+            return lm
+
+        def bounded(c, lm):
+            th = work.tile([P, PACK * CHUNKS[c]], F32, name="th")
             nc.scalar.activation(
                 th[:].rearrange("p (e j h) -> p e j h", e=2, h=2),
                 lm[:].rearrange("p (e h j) -> p e j h", e=2, h=2),
                 ACT.Tanh,
             )
-            mx = work.tile([P, PACK * CHUNK], F32, name="mx")
+            return th
+
+        def rate(c, th):
+            mx = work.tile([P, PACK * CHUNKS[c]], F32, name="mx")
             nc.scalar.activation(mx[:], th[:], ACT.Exp, scale=1.2)
-            alive = work.tile([P, PACK * CHUNK], F32, name="alive")
+            return mx
+
+        def survival(c, mx):
+            alive = work.tile([P, PACK * CHUNKS[c]], F32, name="alive")
             nc.scalar.activation(
                 alive[:].rearrange("p (m e) -> p m e", e=2),
                 mx[:].rearrange("p (e m) -> p m e", e=2),
@@ -200,19 +216,23 @@ def tile_picked_yleeca_imp_p_kernel(tc, x_words, x_scales, w1, w2, bx, gx, unit,
             )
             return alive
 
-        def finish(c, j0, alive):
-            cols = slice(j0, j0 + CHUNK)
-            hid = work.tile([P, PACK * CHUNK], BF16, name="hid", align_bytes=64)
+        def hidden(c, alive):
+            j0, n = starts[c], CHUNKS[c]
+            hid = work.tile([P, PACK * n], BF16, name="hid", align_bytes=64)
             nc.vector.scalar_tensor_tensor(
                 hid[:].rearrange("p (m e) -> p m e", e=2),
                 alive[:].rearrange("p (m e) -> p m e", e=2),
                 1.0,
-                ndk[:, :, 2 * j0 : 2 * (j0 + CHUNK)].rearrange("p e m -> p m e"),
+                ndk[:, :, 2 * j0 : 2 * (j0 + n)].rearrange("p e m -> p m e"),
                 ALU.subtract,
                 ALU.mult,
             )
-            hid_codes, hid_scales = quantize(work, "hid", hid, CHUNK)
-            acc = psum.tile([P, N // P, CHUNK], F32, name="acc%d" % c, tag="ya%d" % c)
+            return hid
+
+        def last_product(c, hid):
+            n = CHUNKS[c]
+            hid_codes, hid_scales = quantize(work, "hid", hid, n)
+            acc = psum.tile([P, N // P, n], F32, name="acc%d" % c, tag="ya%d" % (c % PACK))
             for r in range(N // P):
                 rows = slice(r * P, (r + 1) * P)
                 nc.tensor.matmul_mx(
@@ -224,13 +244,35 @@ def tile_picked_yleeca_imp_p_kernel(tc, x_words, x_scales, w1, w2, bx, gx, unit,
                     start=True,
                     stop=True,
                 )
-            result = work.tile([P, N // P, CHUNK], F32, name="result")
-            nc.scalar.copy(result[:], acc[:])
-            nc.sync.dma_start(out[:, cols].rearrange("(r p) j -> p r j", p=P), result[:])
+            return acc
 
-        starts = list(range(0, S, CHUNK))
-        alives = [rates(j0) for j0 in starts[:2]]
+        def store(c, acc):
+            j0, n = starts[c], CHUNKS[c]
+            result = work.tile([P, N // P, n], F32, name="result")
+            copy = nc.scalar.copy
+            copy(result[:], acc[:])
+            nc.sync.dma_start(out[:, j0 : j0 + n].rearrange("(r p) j -> p r j", p=P), result[:])
+
+        last = len(CHUNKS) - 1
+        lms = [logits(c) for c in range(2)]
         subtract(1, ukp1)
-        alives.extend([rates(j0) for j0 in starts[2:]])
-        for c, j0 in enumerate(starts):
-            finish(c, j0, alives[c])
+        lms.extend([logits(c) for c in range(2, last + 1)])
+
+        alives = []
+        th = bounded(0, lms[0])
+        for c in range(last + 1):
+            mx = rate(c, th)
+            if c < last:
+                th = bounded(c + 1, lms[c + 1])
+            alives.append(survival(c, mx))
+
+        accs = []
+        hid = hidden(0, alives[0])
+        for c in range(last - 1):
+            ahead = hidden(c + 1, alives[c + 1])
+            accs.append(last_product(c, hid))
+            hid = ahead
+        accs.append(last_product(last - 1, hid))
+        accs.append(last_product(last, hidden(last, alives[last])))
+        for c in range(last + 1):
+            store(c, accs[c])

@@ -21,7 +21,7 @@ K_PASS = P * PACK
 PASSES = K // K_PASS
 LIST_COL = 16
 HALF = S // 2
-CHUNKS = [256,128,64,64]
+CHUNKS = [128,128,128,128]
 SLOTS = [(e, h) for e in range(2) for h in range(2)]
 
 
@@ -144,7 +144,7 @@ def tile_picked_yleeca_imp_p_kernel(tc, x_words, x_scales, w1, w2, bx, gx, unit,
             return ukp
 
         def subtract(e, ukp):
-            [nc.gpsimd,nc.gpsimd][e].tensor_tensor(
+            [nc.vector,nc.vector][e].tensor_tensor(
                 ndk[:, e, :].rearrange("p (j h) -> p j h", h=2),
                 ukp[:].rearrange("p (h j) -> p j h", h=2),
                 ukt[e][:].rearrange("p (h j) -> p j h", h=2),
@@ -164,13 +164,13 @@ def tile_picked_yleeca_imp_p_kernel(tc, x_words, x_scales, w1, w2, bx, gx, unit,
         )
         w3_codes, w3_scales = quantize(keep, "w3", w3_grouped, N)
 
-        ndk = keep.tile([P, 2, 2 * S], F32, name="ndk")
+        ndk = keep.tile([P, 2, 2 * S], F32, name="ndk", tag="w2_raw1")
         subtract(0, ukp0)
 
         gya = [keep.tile([P, S], F32, name="gya%d" % t) for t in range(PACK)]
         for e, h in SLOTS:
             t = 2 * h + e
-            scale_out_of_bank(t in [0], gya[t][:], ya_banks[t][:], gx_sb[:, t : t + 1])
+            scale_out_of_bank(t in [3], gya[t][:], ya_banks[t][:], gx_sb[:, t : t + 1])
 
         ukp1 = fetch_previous(1, "gx_sb")
 
@@ -182,7 +182,7 @@ def tile_picked_yleeca_imp_p_kernel(tc, x_words, x_scales, w1, w2, bx, gx, unit,
             lm = work.tile([P, PACK * n], F32, name="lm")
             for u, (e, h) in enumerate(SLOTS):
                 t = 2 * h + e
-                copy = copy_on_scalar if (c, t) in [] else nc.vector.tensor_copy
+                copy = copy_on_scalar if (c, t) in [(0, 0),(1, 0),(2, 0)] else nc.vector.tensor_copy
                 copy(gc[:, u * n : (u + 1) * n], gya[t][:].indirect(coh_sb[:, j0 // LIST_COL : (j0 + n) // LIST_COL]))
             for u, (e, h) in enumerate(SLOTS):
                 t = 2 * h + e
@@ -254,9 +254,9 @@ def tile_picked_yleeca_imp_p_kernel(tc, x_words, x_scales, w1, w2, bx, gx, unit,
             nc.sync.dma_start(out[:, j0 : j0 + n].rearrange("(r p) j -> p r j", p=P), result[:])
 
         last = len(CHUNKS) - 1
-        lms = [logits(c) for c in range(2)]
+        lms = [logits(c) for c in range(4)]
         subtract(1, ukp1)
-        lms.extend([logits(c) for c in range(2, last + 1)])
+        lms.extend([logits(c) for c in range(4, last + 1)])
 
         alives = []
         th = bounded(0, lms[0])

from contextlib import ExitStack

import concourse.mybir as mybir

K, T, S, N, H = 1024, 2048, 512, 256, 512
FLOPS = 2 * K * H * S * 2 + 2 * H * N * S

F32 = mybir.dt.float32
BF16 = mybir.dt.bfloat16
I32 = mybir.dt.int32
U32 = mybir.dt.uint32
U16 = mybir.dt.uint16
U8 = mybir.dt.uint8
FP8X4 = mybir.dt.float8_e4m3fn_x4
ACT = mybir.ActivationFunctionType
ALU = mybir.AluOpType

P = 128
PACK = 4
K_PASS = P * PACK
PASSES = K // K_PASS
LIST_COL = 16
HALF = S // 2
CHUNKS = [128,128,128,128]
SLOTS = [(e, h) for e in range(2) for h in range(2)]


def tile_picked_yleeca_imp_p_kernel(tc, x_words, x_scales, w1, w2, bx, gx, unit, w3, offs, prv, coh, out):
    nc = tc.nc
    with ExitStack() as ctx:
        lists = ctx.enter_context(tc.tile_pool(name="lists", bufs=1))
        keep = ctx.enter_context(tc.tile_pool(name="keep", bufs=1))
        work = ctx.enter_context(tc.tile_pool(name="work", bufs=len(CHUNKS)))
        psum = ctx.enter_context(tc.psum_pool(name="psum", bufs=1))

        def load_list(name, source):
            tile = lists.tile([P, S // LIST_COL], U16, name=name)
            nc.sync.dma_start(tile[:], source)
            return tile

        def load_rows(name, rows):
            raw = keep.tile([P, PACK, rows.shape[1]], F32, name=name, tag=name)
            nc.sync.dma_start(raw[:], rows.rearrange("(p j) c -> p j c", j=PACK))
            return raw

        def load_words(o):
            table = keep.tile([P, T], U32, name="x_table%d" % o)
            nc.sync.dma_start(table[:].bitcast(I32), x_words[o].rearrange("p c r -> p (c r)").bitcast(I32))
            return table

        def load_factor(name, column):
            tile = keep.tile([P, PACK], F32, name=name, tag=name)
            nc.sync.dma_start(tile[:], column.rearrange("(p t) o -> p (t o)", t=PACK))
            return tile

        def quantize(pool, name, grouped, width):
            codes = pool.tile([P, width], U32, name=name + "_codes", align_bytes=64)
            scales = pool.tile([P, width], U8, name=name + "_scales", align_bytes=64)
            nc.vector.quantize_mx(out=codes[:].bitcast(FP8X4), scales=scales[:], in_=grouped[:])
            return codes, scales

        def copy_on_scalar(out, in_):
            nc.scalar.activation(out, in_, ACT.Copy)

        def scale_out_of_bank(on_vector, out_tile, bank, factor):
            if on_vector:
                nc.vector.tensor_scalar(out_tile, bank, factor, None, ALU.mult)
            else:
                nc.scalar.activation(out_tile, bank, ACT.Copy, scale=factor)

        def quantize_dealt(name, raw, copy):
            grouped = keep.tile([P, H * PACK], BF16, name=name + "_grouped", align_bytes=64)
            copy(
                grouped[:].rearrange("p (t m j) -> p m j t", t=PACK, j=PACK),
                raw[:].rearrange("p j (m t) -> p m j t", t=PACK),
            )
            return quantize(keep, name, grouped, H)

        scale_table = keep.tile([P, T], U8, name="scale_table")
        nc.gpsimd.memset(scale_table[:].bitcast(I32), 0)
        w1_raw = [load_rows("w1_raw0", w1[:K_PASS, :])]
        for q in range(4):
            nc.sync.dma_start(
                scale_table[32 * q : 32 * q + 4 * PASSES, :].bitcast(I32),
                x_scales[:, 4 * q : 4 * q + 4, :].bitcast(I32),
            )
        offs_sb = load_list("offs_sb", offs)
        w1_raw.append(load_rows("w1_raw1", w1[K_PASS:, :]))
        x_tables = [load_words(o) for o in range(PASSES)]
        unit_sb = load_factor("unit_sb", unit)
        prv_sb = load_list("prv_sb", prv)
        w2_raw = [load_rows("w2_raw0", w2[:K_PASS, :])]
        gx_sb = load_factor("gx_sb", gx)
        bx_sb = load_factor("bx_sb", bx)
        w2_raw.append(load_rows("w2_raw1", w2[K_PASS:, :]))
        coh_sb = load_list("coh_sb", coh)
        w3_raw = load_rows("w3_raw", w3)

        x_planes = keep.tile([P, S], U8, name="x_planes", align_bytes=64)
        nc.vector.tensor_copy(x_planes[:], scale_table[:].indirect(offs_sb[:]))
        w1_mx = [
            quantize_dealt("w1_0", w1_raw[0], nc.vector.tensor_copy),
            quantize_dealt("w1_1", w1_raw[1], copy_on_scalar),
        ]
        x_codes = []
        for o in range(PASSES):
            picked = keep.tile([P, S], U32, name="x_codes%d" % o, align_bytes=64)
            nc.vector.tensor_copy(picked[:], x_tables[o][:].indirect(offs_sb[:]))
            x_codes.append(picked)

        def product_pass(banks, w_mx, o):
            codes, scales = w_mx
            for e, h in SLOTS:
                t = 2 * h + e
                cols = slice(t * P, (t + 1) * P)
                nc.tensor.matmul_mx(
                    out=banks[t][:],
                    lhsT=codes[:, cols].bitcast(FP8X4),
                    lhsT_scale=scales[:, cols],
                    rhs=x_codes[o][:].bitcast(FP8X4),
                    rhs_scale=x_planes[4 * o : P, :],
                    start=(o == 0),
                    stop=(o == PASSES - 1),
                )

        kt_banks = [psum.tile([P, S], F32, name="kt%d" % t) for t in range(PACK)]
        for o in range(PASSES):
            product_pass(kt_banks, w1_mx[o], o)

        ukt = [keep.tile([P, 2 * S], F32, name="ukt%d" % e) for e in range(2)]
        for e, h in SLOTS:
            t = 2 * h + e
            nc.scalar.activation(ukt[e][:, h * S : (h + 1) * S], kt_banks[t][:], ACT.Copy, scale=unit_sb[:, t : t + 1])

        def fetch_previous(e, tag):
            ukp = keep.tile([P, 2 * S], F32, name="ukp%d" % e, tag=tag)
            for h in range(2):
                for j0 in range(0, S, HALF):
                    nc.scalar.activation(
                        ukp[:, h * S + j0 : h * S + j0 + HALF],
                        ukt[e][:, h * S : (h + 1) * S].indirect(prv_sb[:, j0 // LIST_COL : (j0 + HALF) // LIST_COL]),
                        ACT.Copy,
                    )
            return ukp

        def subtract(e, ukp):
            [nc.vector,nc.vector][e].tensor_tensor(
                ndk[:, e, :].rearrange("p (j h) -> p j h", h=2),
                ukp[:].rearrange("p (h j) -> p j h", h=2),
                ukt[e][:].rearrange("p (h j) -> p j h", h=2),
                ALU.subtract,
            )

        ukp0 = fetch_previous(0, "ukp0")

        ya_banks = [psum.tile([P, S], F32, name="ya%d" % t, tag="ya%d" % t) for t in range(PACK)]
        for o in range(PASSES):
            product_pass(ya_banks, quantize_dealt("w2_%d" % o, w2_raw[o], nc.vector.tensor_copy), o)

        w3_grouped = keep.tile([P, N * PACK], BF16, name="w3_grouped", align_bytes=64)
        nc.vector.tensor_copy(
            out=w3_grouped[:].rearrange("p (c i j) -> p c j i", i=4, j=PACK),
            in_=w3_raw[:].rearrange("p j (c i) -> p c j i", i=4),
        )
        w3_codes, w3_scales = quantize(keep, "w3", w3_grouped, N)

        ndk = keep.tile([P, 2, 2 * S], F32, name="ndk", tag="w2_raw1")
        subtract(0, ukp0)

        gya = [keep.tile([P, S], F32, name="gya%d" % t) for t in range(PACK)]
        for e, h in SLOTS:
            t = 2 * h + e
            scale_out_of_bank(t in [3], gya[t][:], ya_banks[t][:], gx_sb[:, t : t + 1])

        ukp1 = fetch_previous(1, "gx_sb")

        starts = [sum(CHUNKS[:c]) for c in range(len(CHUNKS))]

        def logits(c):
            j0, n = starts[c], CHUNKS[c]
            gc = work.tile([P, PACK * n], F32, name="gc")
            lm = work.tile([P, PACK * n], F32, name="lm")
            for u, (e, h) in enumerate(SLOTS):
                t = 2 * h + e
                copy = copy_on_scalar if (c, t) in [(0, 0),(1, 0),(2, 0)] else nc.vector.tensor_copy
                copy(gc[:, u * n : (u + 1) * n], gya[t][:].indirect(coh_sb[:, j0 // LIST_COL : (j0 + n) // LIST_COL]))
            for u, (e, h) in enumerate(SLOTS):
                t = 2 * h + e
                part = slice(u * n, (u + 1) * n)
                nc.vector.scalar_tensor_tensor(
                    lm[:, part], kt_banks[t][:, j0 : j0 + n], bx_sb[:, t : t + 1], gc[:, part], ALU.mult, ALU.add
                )
            return lm

        def bounded(c, lm):
            th = work.tile([P, PACK * CHUNKS[c]], F32, name="th")
            nc.scalar.activation(
                th[:].rearrange("p (e j h) -> p e j h", e=2, h=2),
                lm[:].rearrange("p (e h j) -> p e j h", e=2, h=2),
                ACT.Tanh,
            )
            return th

        def rate(c, th):
            mx = work.tile([P, PACK * CHUNKS[c]], F32, name="mx")
            nc.scalar.activation(mx[:], th[:], ACT.Exp, scale=1.2)
            return mx

        def survival(c, mx):
            alive = work.tile([P, PACK * CHUNKS[c]], F32, name="alive")
            nc.scalar.activation(
                alive[:].rearrange("p (m e) -> p m e", e=2),
                mx[:].rearrange("p (e m) -> p m e", e=2),
                ACT.Exp,
                scale=-1.0,
            )
            return alive

        def hidden(c, alive):
            j0, n = starts[c], CHUNKS[c]
            hid = work.tile([P, PACK * n], BF16, name="hid", align_bytes=64)
            nc.vector.scalar_tensor_tensor(
                hid[:].rearrange("p (m e) -> p m e", e=2),
                alive[:].rearrange("p (m e) -> p m e", e=2),
                1.0,
                ndk[:, :, 2 * j0 : 2 * (j0 + n)].rearrange("p e m -> p m e"),
                ALU.subtract,
                ALU.mult,
            )
            return hid

        def last_product(c, hid):
            n = CHUNKS[c]
            hid_codes, hid_scales = quantize(work, "hid", hid, n)
            acc = psum.tile([P, N // P, n], F32, name="acc%d" % c, tag="ya%d" % (c % PACK))
            for r in range(N // P):
                rows = slice(r * P, (r + 1) * P)
                nc.tensor.matmul_mx(
                    out=acc[:, r, :],
                    lhsT=w3_codes[:, rows].bitcast(FP8X4),
                    lhsT_scale=w3_scales[:, rows],
                    rhs=hid_codes[:].bitcast(FP8X4),
                    rhs_scale=hid_scales[:],
                    start=True,
                    stop=True,
                )
            return acc

        def store(c, acc):
            j0, n = starts[c], CHUNKS[c]
            result = work.tile([P, N // P, n], F32, name="result")
            copy = nc.scalar.copy
            copy(result[:], acc[:])
            nc.sync.dma_start(out[:, j0 : j0 + n].rearrange("(r p) j -> p r j", p=P), result[:])

        last = len(CHUNKS) - 1
        lms = [logits(c) for c in range(4)]
        subtract(1, ukp1)
        lms.extend([logits(c) for c in range(4, last + 1)])

        alives = []
        th = bounded(0, lms[0])
        for c in range(last + 1):
            mx = rate(c, th)
            if c < last:
                th = bounded(c + 1, lms[c + 1])
            alives.append(survival(c, mx))

        accs = []
        hid = hidden(0, alives[0])
        for c in range(last - 1):
            ahead = hidden(c + 1, alives[c + 1])
            accs.append(last_product(c, hid))
            hid = ahead
        accs.append(last_product(last - 1, hid))
        accs.append(last_product(last, hidden(last, alives[last])))
        for c in range(last + 1):
            store(c, accs[c])
